import numpy as np
import ml_dtypes


def mxq(x, axis, fmt="e4m3"):
    dtype, down = {"e4m3": (ml_dtypes.float8_e4m3fn, 7), "e5m2": (ml_dtypes.float8_e5m2, 14)}[fmt]
    v = np.moveaxis(np.asarray(x, np.float32).astype(ml_dtypes.bfloat16).astype(np.float64), axis, -1)
    blocks = v.reshape(v.shape[:-1] + (-1, 32))
    amax = np.abs(blocks).max(-1, keepdims=True)
    byte = np.maximum(np.where(amax > 0, np.frexp(amax)[1] - 1 + 127, 0) - down, 1)
    scale = np.exp2(byte - 127.0)
    codes = (blocks / scale).astype(np.float32).astype(dtype).astype(np.float64)
    return np.moveaxis((codes * scale).reshape(v.shape), -1, axis)


WIDE = False


def mx_kscale(k):
    if not WIDE:
        return np.ones(k)
    levels = np.array([10, -10, 5, -5, 0])
    if k % 512:
        return np.exp2(np.random.permutation(np.resize(levels, k // 32))).repeat(32)
    a = np.empty((k // 512, 16))
    for p in range(k // 512):
        a[p, :8] = np.random.permutation(np.resize(levels, 8))
        for g in range(8):
            far = levels[np.abs(levels - a[p, g]) >= 10]
            a[p, g + 8] = far[np.random.randint(len(far))]
    return np.exp2(a.ravel()).repeat(32)


def f64(x):
    return np.asarray(x).astype(np.float64)


def striped(idx):
    return np.tile(idx.reshape(-1, 16).T, (8, 1)).astype(np.uint16)


def unstriped(offs):
    return offs[:16].T.reshape(-1).astype(np.int64)


E2M1 = np.array([0.0, 0.5, 1.0, 1.5, 2.0, 3.0, 4.0, 6.0, -0.0, -0.5, -1.0, -1.5, -2.0, -3.0, -4.0, -6.0])


def pack_weight(w, fmt):
    k, n = w.shape
    w = f64(np.asarray(w, np.float32).astype(ml_dtypes.bfloat16)).reshape(k // 32, 32, n)
    amax = np.abs(w).max(1)
    if fmt == "e4m3":
        byte = np.frexp(amax)[1] - 1 + 127 - 7
    else:
        mant, ex = np.frexp(amax / 6.0)
        byte = np.where(mant > 0.5, ex, ex - 1) + 127
    byte = np.clip(np.where(amax > 0, byte, 1), 1, 254)
    scaled = (w * np.exp2(127.0 - byte)[:, None, :]).reshape(k, n).astype(np.float32)
    by_word = np.ascontiguousarray(scaled.reshape(k // 512, 128, 4, n).transpose(0, 1, 3, 2))
    if fmt == "e4m3":
        words = by_word.astype(ml_dtypes.float8_e4m3fn).view(np.uint8)
    else:
        c = by_word.astype(ml_dtypes.float4_e2m1fn).view(np.uint8) & 0xF
        words = (c[..., 0::2] | (c[..., 1::2] << 4)).reshape(k // 512, 128, 2 * n)
    return np.ascontiguousarray(words), np.ascontiguousarray(byte.astype(np.uint8).reshape(k // 512, 16, n))


def unpack_weight(words, scales, fmt):
    g, _, n = scales.shape
    words = np.ascontiguousarray(words).reshape(g, 128, n, -1)
    if fmt == "e4m3":
        vals = words.view(ml_dtypes.float8_e4m3fn).astype(np.float64)
    else:
        nib = np.empty((g, 128, n, 4), np.uint8)
        nib[..., 0::2] = words & 0xF
        nib[..., 1::2] = words >> 4
        vals = E2M1[nib]
    vals = vals * np.repeat(np.exp2(scales.astype(np.float64) - 127.0), 8, axis=1)[..., None]
    return vals.transpose(0, 1, 3, 2).reshape(g * 512, n)


def gelu(v):
    return 0.5 * v * (1.0 + np.tanh(np.sqrt(2.0 / np.pi) * (v + 0.044715 * v**3)))


K, T, S, H, P, N2, N3 = 1024, 2048, 1024, 1024, 512, 512, 512

def setup_inputs():
    n = np.random.standard_normal
    s = mx_kscale(K)[:, None]
    u = mx_kscale(H)[:, None]
    d = {}
    d["tab_words"], d["tab_scales"] = pack_weight(n((K, T)) * s, "e2m1")
    d["offs"] = striped(np.random.permutation(T)[:S])
    d["pos1"] = striped(np.random.permutation(S)[:P])
    d["pos2"] = striped(np.random.permutation(S)[:P])
    d["w1"] = (n((K, H)) / s * 1.5 / K**0.5).astype(np.float32)
    d["gain"] = (np.exp(0.3 * n(H)) * u[:, 0]).astype(np.float32)
    d["blend"] = np.random.uniform(-0.25, 1.25, (H, P)).astype(np.float32)
    d["w2_words"], d["w2_scales"] = pack_weight(n((H, N2)) / u * 1.8 / H**0.5, "e2m1")
    d["w3"] = (n((H, N3)) / u * 3.0 / H**0.5).astype(np.float32)
    return d

def reference(tab_words, tab_scales, offs, pos1, pos2, w1, gain, blend, w2_words, w2_scales, w3):
    v = unpack_weight(tab_words, tab_scales, "e2m1")[:, unstriped(offs)]
    h = np.tanh(mxq(f64(w1), 0, "e4m3").T @ v) * f64(gain)[:, None]
    prev = h[:, unstriped(pos1)]
    nxt = h[:, unstriped(pos2)]
    z = nxt + f64(blend) * (prev - nxt)
    zq = mxq(z, 0, "e4m3")
    y2 = unpack_weight(w2_words, w2_scales, "e2m1").T @ zq
    flats = 0.5 * y2 * (1.0 + np.tanh(np.sqrt(2.0 / np.pi) * (y2 + 0.044715 * y2**3)))
    y3 = mxq(f64(w3), 0, "e4m3").T @ zq
    inks = 1.0 / (1.0 + np.exp(-y3))
    return np.concatenate([flats, inks], axis=0)

@@ -1,0 +1,267 @@
+from contextlib import ExitStack
+
+import concourse.mybir as mybir
+
+K, T, S, H, PAIRS, N2, N3 = 1024, 2048, 1024, 1024, 512, 512, 512
+FLOPS = 2 * K * H * S + 2 * H * (N2 + N3) * PAIRS
+
+F32 = mybir.dt.float32
+BF16 = mybir.dt.bfloat16
+I32 = mybir.dt.int32
+U32 = mybir.dt.uint32
+U16 = mybir.dt.uint16
+U8 = mybir.dt.uint8
+FP8X4 = mybir.dt.float8_e4m3fn_x4
+FP4X4 = mybir.dt.float4_e2m1fn_x4
+ACT = mybir.ActivationFunctionType
+ALU = mybir.AluOpType
+
+P = 128
+PACK = 4
+PASS = P * PACK
+BANK = 512
+CHUNKS = ((0, 256), (256, 128), (384, 128))
+
+
+def tile_list_panel_transition_inks_kernel(
+    tc, tab_words, tab_scales, offs, pos1, pos2, w1, gain, blend, w2_words, w2_scales, w3, out
+):
+    nc = tc.nc
+    with ExitStack() as ctx:
+        lists = ctx.enter_context(tc.tile_pool(name="lists", bufs=1))
+        sb = ctx.enter_context(tc.tile_pool(name="sb", bufs=1))
+        psum = ctx.enter_context(tc.psum_pool(name="psum", bufs=1))
+
+        def tile(name, shape, dtype, tag=None):
+            return sb.tile(shape, dtype, name=name, tag=tag or name, align_bytes=64)
+
+        def bank(i, name):
+            return psum.tile([P, BANK], F32, name=name, tag="bank%d" % i)
+
+        offs_t = lists.tile([P, S // 16], U16, name="offs_t")
+        pos1_t = lists.tile([P, PAIRS // 16], U16, name="pos1_t")
+        pos2_t = lists.tile([P, PAIRS // 16], U16, name="pos2_t")
+
+        tabw = [tile("tabw%d" % a, [P, T], U16) for a in range(2)]
+        tabs = [tile("tabs%d" % a, [P, T], U8) for a in range(2)]
+        w2s = tile("w2s", [P, 2 * N2], U8)
+        for a in range(2):
+            nc.vector.memset(tabs[a][:].bitcast(I32), 0)
+        nc.gpsimd.memset(w2s[:].bitcast(I32), 0)
+
+        def load_w1(a, b, c0, c1, name, tag=None):
+            raw = tile(name, [P, PACK, c1 - c0], F32, tag)
+            nc.sync.dma_start(
+                out=raw[:],
+                in_=w1[PASS * a : PASS * (a + 1), PASS * b + c0 : PASS * b + c1].rearrange("(p j) c -> p j c", j=PACK),
+            )
+            return raw
+
+        def load_blend(b):
+            t = tile("blend%d" % b, [P, PACK * PAIRS], F32)
+            nc.sync.dma_start(out=t[:], in_=blend[PASS * b : PASS * (b + 1), :].rearrange("(p t) j -> p (t j)", t=PACK))
+            return t
+
+        nc.sync.dma_start(out=offs_t[:], in_=offs)
+        nc.sync.dma_start(out=tabw[0][:].bitcast(I32), in_=tab_words[0].bitcast(I32))
+
+        def load_scales(a):
+            for q in range(4):
+                nc.sync.dma_start(
+                    out=tabs[a][32 * q : 32 * q + 4, :].bitcast(I32), in_=tab_scales[a, 4 * q : 4 * q + 4, :].bitcast(I32)
+                )
+
+        load_scales(0)
+        raw00 = load_w1(0, 0, 0, PASS, "raw00")
+        load_scales(1)
+        nc.sync.dma_start(out=tabw[1][:].bitcast(I32), in_=tab_words[1].bitcast(I32))
+        raw10 = [load_w1(1, 0, 256 * u, 256 * (u + 1), "raw10_%d" % u) for u in range(2)]
+        g = tile("g", [P, 2, PACK], F32)
+        nc.sync.dma_start(out=g[:], in_=gain.rearrange("(b p t) -> p b t", b=2, t=PACK))
+        nc.sync.dma_start(out=pos1_t[:], in_=pos1)
+        nc.sync.dma_start(out=pos2_t[:], in_=pos2)
+        wa = [load_blend(0)]
+        raw01 = load_w1(0, 1, 0, PASS, "raw01")
+        raw11 = load_w1(1, 1, 0, PASS, "raw11")
+        wa.append(load_blend(1))
+
+        def cast_w1(raw, grouped, m0, m1):
+            nc.scalar.activation(
+                out=grouped[:].rearrange("p (t m j) -> p m j t", t=PACK, j=PACK)[:, m0:m1],
+                in_=raw[:].rearrange("p j (m t) -> p m j t", t=PACK),
+                func=ACT.Copy,
+            )
+
+        def quantise(name, grouped, width):
+            codes = tile(name + "_c", [P, width], U32)
+            scales = tile(name + "_s", [P, width], U8)
+            nc.vector.quantize_mx(out=codes[:].bitcast(FP8X4), scales=scales[:], in_=grouped[:])
+            return codes, scales
+
+        vw = {}
+
+        def gather_words(a):
+            for u in range(2):
+                t = tile("vw%d%d" % (a, u), [P, BANK], U16)
+                nc.vector.tensor_copy(out=t[:], in_=tabw[a][:].indirect(offs_t[:, 32 * u : 32 * (u + 1)]))
+                vw[a, u] = t
+
+        gather_words(0)
+        planes = [tile("plane%d" % a, [P, S], U8) for a in range(2)]
+        for a in range(2):
+            nc.vector.tensor_copy(out=planes[a][:], in_=tabs[a][:].indirect(offs_t[:]))
+        gb00 = tile("gb00", [P, PACK * PASS], BF16)
+        cast_w1(raw00, gb00, 0, P)
+        gather_words(1)
+        w1q = {}
+        w1q[0, 0] = quantise("w1q00", gb00, PASS)
+        gb10 = tile("gb10", [P, PACK * PASS], BF16)
+        for u in range(2):
+            cast_w1(raw10[u], gb10, 64 * u, 64 * (u + 1))
+        w1q[1, 0] = quantise("w1q10", gb10, PASS)
+
+        ng = tile("ng", [P, 2, PACK], F32)
+        nc.vector.tensor_scalar(out=ng[:], in0=g[:], scalar1=-1.0, scalar2=None, op0=ALU.mult)
+
+        h = {}
+
+        def features(b, t):
+            ht = tile("h%d%d" % (b, t), [P, S], F32)
+            for u in range(2):
+                acc = bank(2 * t + u, "acc%d%d%d" % (b, t, u))
+                for a in range(2):
+                    codes, scales = w1q[a, b]
+                    nc.tensor.matmul_mx(
+                        out=acc[:],
+                        lhsT=codes[:, P * t : P * (t + 1)].bitcast(FP8X4),
+                        lhsT_scale=scales[:, P * t : P * (t + 1)],
+                        rhs=vw[a, u][:].bitcast(FP4X4),
+                        rhs_scale=planes[a][:, BANK * u : BANK * (u + 1)],
+                        start=(a == 0),
+                        stop=(a == 1),
+                    )
+                nc.scalar.activation(out=ht[:, BANK * u : BANK * (u + 1)], in_=acc[:], func=ACT.Tanh)
+            h[b, t] = ht
+
+        wb = [tile("wb%d" % b, [P, PACK * PAIRS], F32) for b in range(2)]
+
+        def weights(b, t):
+            cols = slice(PAIRS * t, PAIRS * (t + 1))
+            gt, ngt = g[:, b, t : t + 1], ng[:, b, t : t + 1]
+            if b == 0:
+                nc.vector.tensor_scalar(out=wb[b][:, cols], in0=wa[b][:, cols], scalar1=ngt, scalar2=gt, op0=ALU.mult, op1=ALU.add)
+                nc.vector.tensor_scalar(out=wa[b][:, cols], in0=wa[b][:, cols], scalar1=gt, scalar2=None, op0=ALU.mult)
+            else:
+                nc.scalar.activation(out=wb[b][:, cols], in_=wa[b][:, cols], func=ACT.Identity, bias=gt, scale=ngt)
+                nc.scalar.activation(out=wa[b][:, cols], in_=wa[b][:, cols], func=ACT.Copy, scale=gt)
+
+        def picks(b, t, j0, width, prev, nxt):
+            src = slice(PAIRS * t + j0, PAIRS * t + j0 + width)
+            dst = slice(width * t, width * (t + 1))
+            lst = slice(j0 // 16, (j0 + width) // 16)
+            nc.vector.tensor_tensor(out=prev[:, dst], in0=h[b, t][:].indirect(pos1_t[:, lst]), in1=wa[b][:, src], op=ALU.mult)
+            nc.vector.tensor_tensor(out=nxt[:, dst], in0=h[b, t][:].indirect(pos2_t[:, lst]), in1=wb[b][:, src], op=ALU.mult)
+
+        def join(name, width, prev, nxt):
+            zb = tile(name + "_b", [P, PACK * width], BF16)
+            nc.vector.tensor_tensor(
+                out=zb[:].rearrange("p (c i t) -> p c t i", i=4, t=PACK),
+                in0=prev[:].rearrange("p (t c i) -> p c t i", t=PACK, i=4),
+                in1=nxt[:].rearrange("p (t c i) -> p c t i", t=PACK, i=4),
+                op=ALU.add,
+            )
+            return quantise(name, zb, width)
+
+        prev0 = tile("prev0", [P, PACK * PAIRS], F32)
+        nxt0 = tile("nxt0", [P, PACK * PAIRS], F32)
+        for t in range(PACK):
+            features(0, t)
+            weights(0, t)
+            picks(0, t, 0, PAIRS, prev0, nxt0)
+            if t in (1, 2):
+                a = t - 1
+                gb = tile("gb%d1" % a, [P, PACK * PASS], BF16)
+                cast_w1((raw01, raw11)[a], gb, 0, P)
+                w1q[a, 1] = quantise("w1q%d1" % a, gb, PASS)
+        zq0 = join("z0", PAIRS, prev0, nxt0)
+
+        raw3 = []
+        for a in range(2):
+            raw = tile("raw3_%d" % a, [P, PACK, N3], F32, "raw00" if a == 0 else None)
+            nc.sync.dma_start(out=raw[:], in_=w3[PASS * a : PASS * (a + 1), :].rearrange("(p j) n -> p j n", j=PACK))
+            raw3.append(raw)
+        w2w = tile("w2w", [P, 2, 2 * N2], U8)
+        nc.sync.dma_start(out=w2w[:].bitcast(I32), in_=w2_words.rearrange("a p c -> p a c").bitcast(I32))
+        for q in range(4):
+            nc.sync.dma_start(
+                out=w2s[32 * q : 32 * q + 4, :].rearrange("r (a n) -> r a n", a=2).bitcast(I32),
+                in_=w2_scales[:, 4 * q : 4 * q + 4, :].rearrange("a r n -> r a n").bitcast(I32),
+            )
+
+        for t in range(PACK):
+            weights(1, t)
+            features(1, t)
+
+        w3q = []
+        for a in range(2):
+            gb = tile("gb3_%d" % a, [P, PACK * N3], BF16, "hold%d" % a)
+            nc.scalar.activation(
+                out=gb[:].rearrange("p (c i j) -> p c j i", i=4, j=PACK),
+                in_=raw3[a][:].rearrange("p j (c i) -> p c j i", i=4),
+                func=ACT.Copy,
+            )
+            w3q.append(quantise("w3q%d" % a, gb, N3))
+
+        def second(kind, n, a, acc, c0, zq, z0, width, start, stop):
+            codes, scales = zq
+            if kind == 0:
+                lhsT = w2w[:, a, 2 * P * n : 2 * P * (n + 1)].bitcast(FP4X4)
+                lhsT_scale = w2s[:, N2 * a + P * n : N2 * a + P * (n + 1)]
+            else:
+                lhsT = w3q[a][0][:, P * n : P * (n + 1)].bitcast(FP8X4)
+                lhsT_scale = w3q[a][1][:, P * n : P * (n + 1)]
+            nc.tensor.matmul_mx(
+                out=acc[:, c0 : c0 + width],
+                lhsT=lhsT,
+                lhsT_scale=lhsT_scale,
+                rhs=codes[:, z0 : z0 + width].bitcast(FP8X4),
+                rhs_scale=scales[:, z0 : z0 + width],
+                start=start,
+                stop=stop,
+            )
+
+        groups = []
+        for c, (j0, width) in enumerate(CHUNKS):
+            per = BANK // width
+            for kind in (1, 0):
+                for n0 in range(0, 4, per):
+                    acc = bank(len(groups), "out%d%d%d" % (c, kind, n0))
+                    groups.append((c, kind, n0, per, acc))
+                    for k in range(per):
+                        second(kind, n0 + k, 0, acc, width * k, zq0, j0, width, k == 0, False)
+
+        for c, (j0, width) in enumerate(CHUNKS):
+            prev = tile("prev1_%d" % c, [P, PACK * width], F32, None if c == 0 else "hold%d" % (c - 1))
+            nxt = tile("nxt1_%d" % c, [P, PACK * width], F32)
+            for t in range(PACK):
+                picks(1, t, j0, width, prev, nxt)
+            zq1 = join("z1_%d" % c, width, prev, nxt)
+            for gc, kind, n0, per, acc in groups:
+                if gc != c:
+                    continue
+                for k in range(per):
+                    second(kind, n0 + k, 1, acc, width * k, zq1, 0, width, False, k == per - 1)
+                res = tile("res%d%d%d" % (c, kind, n0), [P, BANK], F32)
+                if kind == 0:
+                    nc.scalar.activation(out=res[:], in_=acc[:], func=ACT.Gelu_apprx_tanh)
+                else:
+                    nc.scalar.activation(out=res[:], in_=acc[:], func=ACT.Tanh, scale=0.5)
+                    if c == len(CHUNKS) - 1:
+                        nc.vector.tensor_scalar(out=res[:], in0=res[:], scalar1=0.5, scalar2=0.5, op0=ALU.mult, op1=ALU.add)
+                    else:
+                        nc.scalar.activation(out=res[:], in_=res[:], func=ACT.Copy, scale=0.5, bias=0.5)
+                row0 = N2 * kind + P * n0
+                nc.sync.dma_start(
+                    out=out[row0 : row0 + P * per, j0 : j0 + width].rearrange("(k p) c -> p k c", p=P),
+                    in_=res[:].rearrange("p (k c) -> p k c", k=per),
+                )

@@ -43,11 +43,17 @@ def tile_list_panel_transition_inks_kernel(
         pos2_t = lists.tile([P, PAIRS // 16], U16, name="pos2_t")
 
         tabw = [tile("tabw%d" % a, [P, T], U16) for a in range(2)]
-        tabs = [tile("tabs%d" % a, [P, T], U8) for a in range(2)]
+        tabs = tile("tabs", [P, T], U8)
+        plane1 = tile("plane1", [P, S], U8)
         w2s = tile("w2s", [P, 2 * N2], U8)
-        for a in range(2):
-            nc.vector.memset(tabs[a][:].bitcast(I32), 0)
+        nc.gpsimd.memset(tabs[:].bitcast(I32), 0)
         nc.gpsimd.memset(w2s[:].bitcast(I32), 0)
+        nc.vector.memset(plane1[:].bitcast(I32), 0)
+        for q in range(4):
+            nc.gpsimd.dma_start(
+                out=w2s[32 * q : 32 * q + 4, :].rearrange("r (a n) -> r a n", a=2).bitcast(I32),
+                in_=w2_scales[:, 4 * q : 4 * q + 4, :].rearrange("a r n -> r a n").bitcast(I32),
+            )
 
         def load_w1(a, b, c0, c1, name, tag=None):
             raw = tile(name, [P, PACK, c1 - c0], F32, tag)
@@ -57,23 +63,18 @@ def tile_list_panel_transition_inks_kernel(
             )
             return raw
 
-        def load_blend(b):
-            t = tile("blend%d" % b, [P, PACK * PAIRS], F32)
+        def load_blend(b, tag=None):
+            t = tile("blend%d" % b, [P, PACK * PAIRS], F32, tag)
             nc.sync.dma_start(out=t[:], in_=blend[PASS * b : PASS * (b + 1), :].rearrange("(p t) j -> p (t j)", t=PACK))
             return t
 
         nc.sync.dma_start(out=offs_t[:], in_=offs)
         nc.sync.dma_start(out=tabw[0][:].bitcast(I32), in_=tab_words[0].bitcast(I32))
-
-        def load_scales(a):
-            for q in range(4):
-                nc.sync.dma_start(
-                    out=tabs[a][32 * q : 32 * q + 4, :].bitcast(I32), in_=tab_scales[a, 4 * q : 4 * q + 4, :].bitcast(I32)
-                )
-
-        load_scales(0)
+        for q in range(4):
+            nc.sync.dma_start(
+                out=tabs[32 * q : 32 * q + 8, :].bitcast(I32), in_=tab_scales[:, 4 * q : 4 * q + 4, :].bitcast(I32)
+            )
         raw00 = load_w1(0, 0, 0, PASS, "raw00")
-        load_scales(1)
         nc.sync.dma_start(out=tabw[1][:].bitcast(I32), in_=tab_words[1].bitcast(I32))
         raw10 = [load_w1(1, 0, 256 * u, 256 * (u + 1), "raw10_%d" % u) for u in range(2)]
         g = tile("g", [P, 2, PACK], F32)
@@ -81,9 +82,6 @@ def tile_list_panel_transition_inks_kernel(
         nc.sync.dma_start(out=pos1_t[:], in_=pos1)
         nc.sync.dma_start(out=pos2_t[:], in_=pos2)
         wa = [load_blend(0)]
-        raw01 = load_w1(0, 1, 0, PASS, "raw01")
-        raw11 = load_w1(1, 1, 0, PASS, "raw11")
-        wa.append(load_blend(1))
 
         def cast_w1(raw, grouped, m0, m1):
             nc.scalar.activation(
@@ -100,25 +98,30 @@ def tile_list_panel_transition_inks_kernel(
 
         vw = {}
 
-        def gather_words(a):
+        def gather_words(a, tag):
+            vw[a] = tile("vw%d" % a, [P, S], U16, tag)
             for u in range(2):
-                t = tile("vw%d%d" % (a, u), [P, BANK], U16)
-                nc.vector.tensor_copy(out=t[:], in_=tabw[a][:].indirect(offs_t[:, 32 * u : 32 * (u + 1)]))
-                vw[a, u] = t
+                nc.vector.tensor_copy(
+                    out=vw[a][:, BANK * u : BANK * (u + 1)], in_=tabw[a][:].indirect(offs_t[:, 32 * u : 32 * (u + 1)])
+                )
 
-        gather_words(0)
-        planes = [tile("plane%d" % a, [P, S], U8) for a in range(2)]
-        for a in range(2):
-            nc.vector.tensor_copy(out=planes[a][:], in_=tabs[a][:].indirect(offs_t[:]))
+        gather_words(0, None)
+        plane0 = tile("plane0", [P, S], U8)
+        nc.vector.tensor_copy(out=plane0[:], in_=tabs[:].indirect(offs_t[:]))
+        nc.sync.dma_start(out=plane1[0:100, :].bitcast(I32), in_=plane0[4:104, :].bitcast(I32))
+        planes = [plane0, plane1]
         gb00 = tile("gb00", [P, PACK * PASS], BF16)
         cast_w1(raw00, gb00, 0, P)
-        gather_words(1)
         w1q = {}
         w1q[0, 0] = quantise("w1q00", gb00, PASS)
+        gather_words(1, "gb00")
         gb10 = tile("gb10", [P, PACK * PASS], BF16)
         for u in range(2):
             cast_w1(raw10[u], gb10, 64 * u, 64 * (u + 1))
         w1q[1, 0] = quantise("w1q10", gb10, PASS)
+        raw01 = load_w1(0, 1, 0, PASS, "raw01", "raw00")
+        raw11 = load_w1(1, 1, 0, PASS, "raw11", "raw10_0")
+        wa.append(load_blend(1, "raw10_1"))
 
         ng = tile("ng", [P, 2, PACK], F32)
         nc.vector.tensor_scalar(out=ng[:], in0=g[:], scalar1=-1.0, scalar2=None, op0=ALU.mult)
@@ -135,7 +138,7 @@ def tile_list_panel_transition_inks_kernel(
                         out=acc[:],
                         lhsT=codes[:, P * t : P * (t + 1)].bitcast(FP8X4),
                         lhsT_scale=scales[:, P * t : P * (t + 1)],
-                        rhs=vw[a, u][:].bitcast(FP4X4),
+                        rhs=vw[a][:, BANK * u : BANK * (u + 1)].bitcast(FP4X4),
                         rhs_scale=planes[a][:, BANK * u : BANK * (u + 1)],
                         start=(a == 0),
                         stop=(a == 1),
@@ -148,7 +151,7 @@ def tile_list_panel_transition_inks_kernel(
         def weights(b, t):
             cols = slice(PAIRS * t, PAIRS * (t + 1))
             gt, ngt = g[:, b, t : t + 1], ng[:, b, t : t + 1]
-            if b == 0:
+            if b == 0 and t < 2:
                 nc.vector.tensor_scalar(out=wb[b][:, cols], in0=wa[b][:, cols], scalar1=ngt, scalar2=gt, op0=ALU.mult, op1=ALU.add)
                 nc.vector.tensor_scalar(out=wa[b][:, cols], in0=wa[b][:, cols], scalar1=gt, scalar2=None, op0=ALU.mult)
             else:
@@ -187,16 +190,11 @@ def tile_list_panel_transition_inks_kernel(
 
         raw3 = []
         for a in range(2):
-            raw = tile("raw3_%d" % a, [P, PACK, N3], F32, "raw00" if a == 0 else None)
+            raw = tile("raw3_%d" % a, [P, PACK, N3], F32, "gb10" if a == 0 else "raw00")
             nc.sync.dma_start(out=raw[:], in_=w3[PASS * a : PASS * (a + 1), :].rearrange("(p j) n -> p j n", j=PACK))
             raw3.append(raw)
-        w2w = tile("w2w", [P, 2, 2 * N2], U8)
+        w2w = tile("w2w", [P, 2, 2 * N2], U8, "gb01")
         nc.sync.dma_start(out=w2w[:].bitcast(I32), in_=w2_words.rearrange("a p c -> p a c").bitcast(I32))
-        for q in range(4):
-            nc.sync.dma_start(
-                out=w2s[32 * q : 32 * q + 4, :].rearrange("r (a n) -> r a n", a=2).bitcast(I32),
-                in_=w2_scales[:, 4 * q : 4 * q + 4, :].rearrange("a r n -> r a n").bitcast(I32),
-            )
 
         for t in range(PACK):
             weights(1, t)

@@ -49,6 +49,8 @@ def tile_list_panel_transition_inks_kernel(
         nc.gpsimd.memset(tabs[:].bitcast(I32), 0)
         nc.gpsimd.memset(w2s[:].bitcast(I32), 0)
         nc.vector.memset(plane1[:].bitcast(I32), 0)
+        g = tile("g", [P, 2, PACK], F32)
+        nc.gpsimd.dma_start(out=g[:], in_=gain.rearrange("(b p t) -> p b t", b=2, t=PACK))
         for q in range(4):
             nc.gpsimd.dma_start(
                 out=w2s[32 * q : 32 * q + 4, :].rearrange("r (a n) -> r a n", a=2).bitcast(I32),
@@ -63,25 +65,28 @@ def tile_list_panel_transition_inks_kernel(
             )
             return raw
 
-        def load_blend(b, tag=None):
-            t = tile("blend%d" % b, [P, PACK * PAIRS], F32, tag)
-            nc.sync.dma_start(out=t[:], in_=blend[PASS * b : PASS * (b + 1), :].rearrange("(p t) j -> p (t j)", t=PACK))
-            return t
+        def load_blend(b, t0, t1, tag=None):
+            rows = tile("blend%d%d" % (b, t0), [P, (t1 - t0) * PAIRS], F32, tag)
+            nc.sync.dma_start(
+                out=rows[:],
+                in_=blend[PASS * b : PASS * (b + 1), :].rearrange("(p t) j -> p (t j)", t=PACK)[:, PAIRS * t0 : PAIRS * t1],
+            )
+            for t in range(t0, t1):
+                wa[b, t] = rows[:, PAIRS * (t - t0) : PAIRS * (t - t0 + 1)]
 
         nc.sync.dma_start(out=offs_t[:], in_=offs)
         nc.sync.dma_start(out=tabw[0][:].bitcast(I32), in_=tab_words[0].bitcast(I32))
-        for q in range(4):
+        for r in range(4):
             nc.sync.dma_start(
-                out=tabs[32 * q : 32 * q + 8, :].bitcast(I32), in_=tab_scales[:, 4 * q : 4 * q + 4, :].bitcast(I32)
+                out=tabs[r:P:16, :].bitcast(I32), in_=tab_scales[:, r:16:4, :].rearrange("a q t -> q a t").bitcast(I32)
             )
         raw00 = load_w1(0, 0, 0, PASS, "raw00")
         nc.sync.dma_start(out=tabw[1][:].bitcast(I32), in_=tab_words[1].bitcast(I32))
         raw10 = [load_w1(1, 0, 256 * u, 256 * (u + 1), "raw10_%d" % u) for u in range(2)]
-        g = tile("g", [P, 2, PACK], F32)
-        nc.sync.dma_start(out=g[:], in_=gain.rearrange("(b p t) -> p b t", b=2, t=PACK))
         nc.sync.dma_start(out=pos1_t[:], in_=pos1)
         nc.sync.dma_start(out=pos2_t[:], in_=pos2)
-        wa = [load_blend(0)]
+        wa = {}
+        load_blend(0, 0, 2)
 
         def cast_w1(raw, grouped, m0, m1):
             nc.scalar.activation(
@@ -90,55 +95,56 @@ def tile_list_panel_transition_inks_kernel(
                 func=ACT.Copy,
             )
 
-        def quantise(name, grouped, width):
+        def quantise(name, grouped, width, cuts=()):
             codes = tile(name + "_c", [P, width], U32)
             scales = tile(name + "_s", [P, width], U8)
-            nc.vector.quantize_mx(out=codes[:].bitcast(FP8X4), scales=scales[:], in_=grouped[:])
+            edges = (0,) + cuts + (width,)
+            for c0, c1 in zip(edges, edges[1:]):
+                nc.vector.quantize_mx(
+                    out=codes[:, c0:c1].bitcast(FP8X4), scales=scales[:, c0:c1], in_=grouped[:, PACK * c0 : PACK * c1]
+                )
             return codes, scales
 
         vw = {}
 
-        def gather_words(a, tag):
-            vw[a] = tile("vw%d" % a, [P, S], U16, tag)
+        def gather_words(a, tags):
             for u in range(2):
-                nc.vector.tensor_copy(
-                    out=vw[a][:, BANK * u : BANK * (u + 1)], in_=tabw[a][:].indirect(offs_t[:, 32 * u : 32 * (u + 1)])
-                )
+                vw[a, u] = tile("vw%d%d" % (a, u), [P, BANK], U16, tags[u])
+                nc.vector.tensor_copy(out=vw[a, u][:], in_=tabw[a][:].indirect(offs_t[:, 32 * u : 32 * (u + 1)]))
 
-        gather_words(0, None)
         plane0 = tile("plane0", [P, S], U8)
         nc.vector.tensor_copy(out=plane0[:], in_=tabs[:].indirect(offs_t[:]))
-        nc.sync.dma_start(out=plane1[0:100, :].bitcast(I32), in_=plane0[4:104, :].bitcast(I32))
+        for r in range(4):
+            nc.sync.dma_start(out=plane1[r:P:32, :].bitcast(I32), in_=plane0[16 + r : P : 32, :].bitcast(I32))
+        load_blend(0, 2, 4, "tabs")
         planes = [plane0, plane1]
+        gather_words(0, (None, None))
         gb00 = tile("gb00", [P, PACK * PASS], BF16)
         cast_w1(raw00, gb00, 0, P)
         w1q = {}
         w1q[0, 0] = quantise("w1q00", gb00, PASS)
-        gather_words(1, "gb00")
+        gather_words(1, (None, "gb00"))
         gb10 = tile("gb10", [P, PACK * PASS], BF16)
         for u in range(2):
             cast_w1(raw10[u], gb10, 64 * u, 64 * (u + 1))
-        w1q[1, 0] = quantise("w1q10", gb10, PASS)
+        w1q[1, 0] = quantise("w1q10", gb10, PASS, (P,))
         raw01 = load_w1(0, 1, 0, PASS, "raw01", "raw00")
         raw11 = load_w1(1, 1, 0, PASS, "raw11", "raw10_0")
-        wa.append(load_blend(1, "raw10_1"))
-
-        ng = tile("ng", [P, 2, PACK], F32)
-        nc.vector.tensor_scalar(out=ng[:], in0=g[:], scalar1=-1.0, scalar2=None, op0=ALU.mult)
+        load_blend(1, 0, 4, "raw10_1")
 
         h = {}
 
         def features(b, t):
             ht = tile("h%d%d" % (b, t), [P, S], F32)
             for u in range(2):
-                acc = bank(2 * t + u, "acc%d%d%d" % (b, t, u))
+                acc = bank((2 * t + u) % 4, "acc%d%d%d" % (b, t, u))
                 for a in range(2):
                     codes, scales = w1q[a, b]
                     nc.tensor.matmul_mx(
                         out=acc[:],
                         lhsT=codes[:, P * t : P * (t + 1)].bitcast(FP8X4),
                         lhsT_scale=scales[:, P * t : P * (t + 1)],
-                        rhs=vw[a][:, BANK * u : BANK * (u + 1)].bitcast(FP4X4),
+                        rhs=vw[a, u][:].bitcast(FP4X4),
                         rhs_scale=planes[a][:, BANK * u : BANK * (u + 1)],
                         start=(a == 0),
                         stop=(a == 1),
@@ -146,47 +152,52 @@ def tile_list_panel_transition_inks_kernel(
                 nc.scalar.activation(out=ht[:, BANK * u : BANK * (u + 1)], in_=acc[:], func=ACT.Tanh)
             h[b, t] = ht
 
-        wb = [tile("wb%d" % b, [P, PACK * PAIRS], F32) for b in range(2)]
+        wb = {}
+        wa0 = tile("wa0", [P, 2 * PAIRS], F32, "gb10")
 
         def weights(b, t):
-            cols = slice(PAIRS * t, PAIRS * (t + 1))
-            gt, ngt = g[:, b, t : t + 1], ng[:, b, t : t + 1]
+            wb[b, t] = tile("wb%d%d" % (b, t), [P, PAIRS], F32)[:]
+            gt = g[:, b, t : t + 1]
             if b == 0 and t < 2:
-                nc.vector.tensor_scalar(out=wb[b][:, cols], in0=wa[b][:, cols], scalar1=ngt, scalar2=gt, op0=ALU.mult, op1=ALU.add)
-                nc.vector.tensor_scalar(out=wa[b][:, cols], in0=wa[b][:, cols], scalar1=gt, scalar2=None, op0=ALU.mult)
+                scaled = wa0[:, PAIRS * t : PAIRS * (t + 1)]
+                nc.vector.tensor_scalar(out=scaled, in0=wa[b, t], scalar1=gt, scalar2=None, op0=ALU.mult)
+                wa[b, t] = scaled
+                nc.vector.tensor_scalar(out=wb[b, t], in0=wa[b, t], scalar1=-1.0, scalar2=gt, op0=ALU.mult, op1=ALU.add)
             else:
-                nc.scalar.activation(out=wb[b][:, cols], in_=wa[b][:, cols], func=ACT.Identity, bias=gt, scale=ngt)
-                nc.scalar.activation(out=wa[b][:, cols], in_=wa[b][:, cols], func=ACT.Copy, scale=gt)
+                nc.scalar.activation(out=wa[b, t], in_=wa[b, t], func=ACT.Copy, scale=gt)
+                nc.scalar.activation(out=wb[b, t], in_=wa[b, t], func=ACT.Identity, bias=gt, scale=-1.0)
 
-        def picks(b, t, j0, width, prev, nxt):
-            src = slice(PAIRS * t + j0, PAIRS * t + j0 + width)
-            dst = slice(width * t, width * (t + 1))
-            lst = slice(j0 // 16, (j0 + width) // 16)
-            nc.vector.tensor_tensor(out=prev[:, dst], in0=h[b, t][:].indirect(pos1_t[:, lst]), in1=wa[b][:, src], op=ALU.mult)
-            nc.vector.tensor_tensor(out=nxt[:, dst], in0=h[b, t][:].indirect(pos2_t[:, lst]), in1=wb[b][:, src], op=ALU.mult)
+        def pick(which, b, t, j0, width, dst):
+            nc.vector.tensor_tensor(
+                out=dst[:, width * t : width * (t + 1)],
+                in0=h[b, t][:].indirect((pos1_t, pos2_t)[which][:, j0 // 16 : (j0 + width) // 16]),
+                in1=(wa, wb)[which][b, t][:, j0 : j0 + width],
+                op=ALU.mult,
+            )
 
         def join(name, width, prev, nxt):
             zb = tile(name + "_b", [P, PACK * width], BF16)
             nc.vector.tensor_tensor(
-                out=zb[:].rearrange("p (c i t) -> p c t i", i=4, t=PACK),
-                in0=prev[:].rearrange("p (t c i) -> p c t i", t=PACK, i=4),
-                in1=nxt[:].rearrange("p (t c i) -> p c t i", t=PACK, i=4),
+                out=zb[:].rearrange("p (c i t) -> p c t i", i=2, t=PACK),
+                in0=prev[:].rearrange("p (t c i) -> p c t i", t=PACK, i=2),
+                in1=nxt[:].rearrange("p (t c i) -> p c t i", t=PACK, i=2),
                 op=ALU.add,
             )
-            return quantise(name, zb, width)
+            return zb
 
         prev0 = tile("prev0", [P, PACK * PAIRS], F32)
         nxt0 = tile("nxt0", [P, PACK * PAIRS], F32)
         for t in range(PACK):
             features(0, t)
             weights(0, t)
-            picks(0, t, 0, PAIRS, prev0, nxt0)
+            pick(0, 0, t, 0, PAIRS, prev0)
+            pick(1, 0, t, 0, PAIRS, nxt0)
             if t in (1, 2):
                 a = t - 1
                 gb = tile("gb%d1" % a, [P, PACK * PASS], BF16)
                 cast_w1((raw01, raw11)[a], gb, 0, P)
                 w1q[a, 1] = quantise("w1q%d1" % a, gb, PASS)
-        zq0 = join("z0", PAIRS, prev0, nxt0)
+        zq0 = quantise("z0", join("z0", PAIRS, prev0, nxt0), PAIRS)
 
         raw3 = []
         for a in range(2):
@@ -233,17 +244,13 @@ def tile_list_panel_transition_inks_kernel(
             per = BANK // width
             for kind in (1, 0):
                 for n0 in range(0, 4, per):
-                    acc = bank(len(groups), "out%d%d%d" % (c, kind, n0))
+                    acc = bank((len(groups) + 4) % 8, "out%d%d%d" % (c, kind, n0))
                     groups.append((c, kind, n0, per, acc))
                     for k in range(per):
                         second(kind, n0 + k, 0, acc, width * k, zq0, j0, width, k == 0, False)
 
-        for c, (j0, width) in enumerate(CHUNKS):
-            prev = tile("prev1_%d" % c, [P, PACK * width], F32, None if c == 0 else "hold%d" % (c - 1))
-            nxt = tile("nxt1_%d" % c, [P, PACK * width], F32)
-            for t in range(PACK):
-                picks(1, t, j0, width, prev, nxt)
-            zq1 = join("z1_%d" % c, width, prev, nxt)
+        def finish(c, zq1):
+            j0, width = CHUNKS[c]
             for gc, kind, n0, per, acc in groups:
                 if gc != c:
                     continue
@@ -263,3 +270,32 @@ def tile_list_panel_transition_inks_kernel(
                     out=out[row0 : row0 + P * per, j0 : j0 + width].rearrange("(k p) c -> p k c", p=P),
                     in_=res[:].rearrange("p (k c) -> p k c", k=per),
                 )
+
+        nxt = [tile("nxt1_%d" % c, [P, PACK * w], F32) for c, (j, w) in enumerate(CHUNKS)]
+
+        def pick1(which, c, t, dst):
+            pick(which, 1, t, CHUNKS[c][0], CHUNKS[c][1], dst)
+
+        prev = tile("prev1_0", [P, PACK * CHUNKS[0][1]], F32)
+        for t in range(PACK):
+            pick1(0, 0, t, prev)
+            pick1(1, 0, t, nxt[0])
+        pick1(1, 1, 0, nxt[1])
+        zb = join("z1_0", CHUNKS[0][1], prev, nxt[0])
+        pick1(1, 1, 1, nxt[1])
+        finish(0, quantise("z1_0", zb, CHUNKS[0][1]))
+        for t in range(2, PACK):
+            pick1(1, 1, t, nxt[1])
+        for t in range(PACK):
+            pick1(1, 2, t, nxt[2])
+        prev = tile("prev1_1", [P, PACK * CHUNKS[1][1]], F32, "hold1")
+        for t in range(PACK):
+            pick1(0, 1, t, prev)
+        zb = join("z1_1", CHUNKS[1][1], prev, nxt[1])
+        prev = tile("prev1_2", [P, PACK * CHUNKS[2][1]], F32, "hold1")
+        pick1(0, 2, 0, prev)
+        finish(1, quantise("z1_1", zb, CHUNKS[1][1]))
+        for t in range(1, PACK):
+            pick1(0, 2, t, prev)
+        zb = join("z1_2", CHUNKS[2][1], prev, nxt[2])
+        finish(2, quantise("z1_2", zb, CHUNKS[2][1]))

@@ -45,17 +45,10 @@ def tile_list_panel_transition_inks_kernel(
         tabw = [tile("tabw%d" % a, [P, T], U16) for a in range(2)]
         tabs = tile("tabs", [P, T], U8)
         plane1 = tile("plane1", [P, S], U8)
-        w2s = tile("w2s", [P, 2 * N2], U8)
         nc.gpsimd.memset(tabs[:].bitcast(I32), 0)
-        nc.gpsimd.memset(w2s[:].bitcast(I32), 0)
         nc.vector.memset(plane1[:].bitcast(I32), 0)
         g = tile("g", [P, 2, PACK], F32)
         nc.gpsimd.dma_start(out=g[:], in_=gain.rearrange("(b p t) -> p b t", b=2, t=PACK))
-        for q in range(4):
-            nc.gpsimd.dma_start(
-                out=w2s[32 * q : 32 * q + 4, :].rearrange("r (a n) -> r a n", a=2).bitcast(I32),
-                in_=w2_scales[:, 4 * q : 4 * q + 4, :].rearrange("a r n -> r a n").bitcast(I32),
-            )
 
         def load_w1(a, b, c0, c1, name, tag=None):
             raw = tile(name, [P, PACK, c1 - c0], F32, tag)
@@ -86,14 +79,15 @@ def tile_list_panel_transition_inks_kernel(
         nc.sync.dma_start(out=pos1_t[:], in_=pos1)
         nc.sync.dma_start(out=pos2_t[:], in_=pos2)
         wa = {}
-        load_blend(0, 0, 2)
+        load_blend(0, 2, 4)
 
         def cast_w1(raw, grouped, m0, m1):
-            nc.scalar.activation(
-                out=grouped[:].rearrange("p (t m j) -> p m j t", t=PACK, j=PACK)[:, m0:m1],
-                in_=raw[:].rearrange("p j (m t) -> p m j t", t=PACK),
-                func=ACT.Copy,
-            )
+            for v in range(2):
+                nc.scalar.activation(
+                    out=grouped[:].rearrange("p (v e m j) -> p v m j e", v=2, e=2, j=PACK)[:, v, m0:m1],
+                    in_=raw[:].rearrange("p j (m v e) -> p v m j e", v=2, e=2)[:, v],
+                    func=ACT.Copy,
+                )
 
         def quantise(name, grouped, width, cuts=()):
             codes = tile(name + "_c", [P, width], U32)
@@ -107,30 +101,34 @@ def tile_list_panel_transition_inks_kernel(
 
         vw = {}
 
-        def gather_words(a, tags):
+        def gather_words(a, tag):
+            vw[a] = tile("vw%d" % a, [P, S], U16, tag)
             for u in range(2):
-                vw[a, u] = tile("vw%d%d" % (a, u), [P, BANK], U16, tags[u])
-                nc.vector.tensor_copy(out=vw[a, u][:], in_=tabw[a][:].indirect(offs_t[:, 32 * u : 32 * (u + 1)]))
+                nc.vector.tensor_copy(
+                    out=vw[a][:, BANK * u : BANK * (u + 1)], in_=tabw[a][:].indirect(offs_t[:, 32 * u : 32 * (u + 1)])
+                )
 
         plane0 = tile("plane0", [P, S], U8)
         nc.vector.tensor_copy(out=plane0[:], in_=tabs[:].indirect(offs_t[:]))
         for r in range(4):
             nc.sync.dma_start(out=plane1[r:P:32, :].bitcast(I32), in_=plane0[16 + r : P : 32, :].bitcast(I32))
-        load_blend(0, 2, 4, "tabs")
         planes = [plane0, plane1]
-        gather_words(0, (None, None))
+        load_blend(0, 0, 2, "tabs")
+        gather_words(0, None)
+        ng = tile("ng", [P, 2, PACK], F32)
+        nc.gpsimd.tensor_scalar(out=ng[:], in0=g[:], scalar1=-1.0, scalar2=None, op0=ALU.mult)
         gb00 = tile("gb00", [P, PACK * PASS], BF16)
         cast_w1(raw00, gb00, 0, P)
         w1q = {}
         w1q[0, 0] = quantise("w1q00", gb00, PASS)
-        gather_words(1, (None, "gb00"))
+        gather_words(1, "gb00")
         gb10 = tile("gb10", [P, PACK * PASS], BF16)
         for u in range(2):
             cast_w1(raw10[u], gb10, 64 * u, 64 * (u + 1))
         w1q[1, 0] = quantise("w1q10", gb10, PASS, (P,))
         raw01 = load_w1(0, 1, 0, PASS, "raw01", "raw00")
         raw11 = load_w1(1, 1, 0, PASS, "raw11", "raw10_0")
-        load_blend(1, 0, 4, "raw10_1")
+        load_blend(1, 0, 4, "tabw1")
 
         h = {}
 
@@ -144,7 +142,7 @@ def tile_list_panel_transition_inks_kernel(
                         out=acc[:],
                         lhsT=codes[:, P * t : P * (t + 1)].bitcast(FP8X4),
                         lhsT_scale=scales[:, P * t : P * (t + 1)],
-                        rhs=vw[a, u][:].bitcast(FP4X4),
+                        rhs=vw[a][:, BANK * u : BANK * (u + 1)].bitcast(FP4X4),
                         rhs_scale=planes[a][:, BANK * u : BANK * (u + 1)],
                         start=(a == 0),
                         stop=(a == 1),
@@ -152,35 +150,36 @@ def tile_list_panel_transition_inks_kernel(
                 nc.scalar.activation(out=ht[:, BANK * u : BANK * (u + 1)], in_=acc[:], func=ACT.Tanh)
             h[b, t] = ht
 
-        wb = {}
-        wa0 = tile("wa0", [P, 2 * PAIRS], F32, "gb10")
+        mix = {}
+        early = tile("early", [P, 4 * PAIRS], F32, "gb10")
 
         def weights(b, t):
-            wb[b, t] = tile("wb%d%d" % (b, t), [P, PAIRS], F32)[:]
-            gt = g[:, b, t : t + 1]
+            gt, ngt = g[:, b, t : t + 1], ng[:, b, t : t + 1]
             if b == 0 and t < 2:
-                scaled = wa0[:, PAIRS * t : PAIRS * (t + 1)]
-                nc.vector.tensor_scalar(out=scaled, in0=wa[b, t], scalar1=gt, scalar2=None, op0=ALU.mult)
-                wa[b, t] = scaled
-                nc.vector.tensor_scalar(out=wb[b, t], in0=wa[b, t], scalar1=-1.0, scalar2=gt, op0=ALU.mult, op1=ALU.add)
+                wp, wn = (early[:, PAIRS * (2 * t + w) : PAIRS * (2 * t + w + 1)] for w in range(2))
+                nc.vector.tensor_scalar(out=wp, in0=wa[b, t], scalar1=gt, scalar2=None, op0=ALU.mult)
+                nc.vector.tensor_scalar(out=wn, in0=wa[b, t], scalar1=ngt, scalar2=gt, op0=ALU.mult, op1=ALU.add)
             else:
-                nc.scalar.activation(out=wa[b, t], in_=wa[b, t], func=ACT.Copy, scale=gt)
-                nc.scalar.activation(out=wb[b, t], in_=wa[b, t], func=ACT.Identity, bias=gt, scale=-1.0)
+                both = tile("mix%d%d" % (b, t), [P, 2 * PAIRS], F32, {(0, 2): "raw10_1", (0, 3): "tabs"}.get((b, t)))
+                wp, wn = both[:, 0:PAIRS], both[:, PAIRS : 2 * PAIRS]
+                nc.scalar.activation(out=wp, in_=wa[b, t], func=ACT.Copy, scale=gt)
+                nc.scalar.activation(out=wn, in_=wa[b, t], func=ACT.Identity, bias=gt, scale=ngt)
+            mix[0, b, t], mix[1, b, t] = wp, wn
 
         def pick(which, b, t, j0, width, dst):
             nc.vector.tensor_tensor(
                 out=dst[:, width * t : width * (t + 1)],
                 in0=h[b, t][:].indirect((pos1_t, pos2_t)[which][:, j0 // 16 : (j0 + width) // 16]),
-                in1=(wa, wb)[which][b, t][:, j0 : j0 + width],
+                in1=mix[which, b, t][:, j0 : j0 + width],
                 op=ALU.mult,
             )
 
-        def join(name, width, prev, nxt):
-            zb = tile(name + "_b", [P, PACK * width], BF16)
+        def join(name, width, prev, nxt, j0, tag=None):
+            zb = tile(name + "_b", [P, PACK * width], BF16, tag)
             nc.vector.tensor_tensor(
                 out=zb[:].rearrange("p (c i t) -> p c t i", i=2, t=PACK),
                 in0=prev[:].rearrange("p (t c i) -> p c t i", t=PACK, i=2),
-                in1=nxt[:].rearrange("p (t c i) -> p c t i", t=PACK, i=2),
+                in1=nxt[:].rearrange("p (t c i) -> p c t i", t=PACK, i=2)[:, j0 // 2 : (j0 + width) // 2],
                 op=ALU.add,
             )
             return zb
@@ -197,14 +196,21 @@ def tile_list_panel_transition_inks_kernel(
                 gb = tile("gb%d1" % a, [P, PACK * PASS], BF16)
                 cast_w1((raw01, raw11)[a], gb, 0, P)
                 w1q[a, 1] = quantise("w1q%d1" % a, gb, PASS)
-        zq0 = quantise("z0", join("z0", PAIRS, prev0, nxt0), PAIRS)
+        zq0 = quantise("z0", join("z0", PAIRS, prev0, nxt0, 0), PAIRS)
 
         raw3 = []
         for a in range(2):
             raw = tile("raw3_%d" % a, [P, PACK, N3], F32, "gb10" if a == 0 else "raw00")
             nc.sync.dma_start(out=raw[:], in_=w3[PASS * a : PASS * (a + 1), :].rearrange("(p j) n -> p j n", j=PACK))
             raw3.append(raw)
-        w2w = tile("w2w", [P, 2, 2 * N2], U8, "gb01")
+        w2s = tile("w2s", [P, 2 * N2], U8, "gb01")
+        nc.gpsimd.memset(w2s[:].bitcast(I32), 0)
+        for q in range(4):
+            nc.sync.dma_start(
+                out=w2s[32 * q : 32 * q + 4, :].rearrange("r (a n) -> r a n", a=2).bitcast(I32),
+                in_=w2_scales[:, 4 * q : 4 * q + 4, :].rearrange("a r n -> r a n").bitcast(I32),
+            )
+        w2w = tile("w2w", [P, 2, 2 * N2], U8, "gb11")
         nc.sync.dma_start(out=w2w[:].bitcast(I32), in_=w2_words.rearrange("a p c -> p a c").bitcast(I32))
 
         for t in range(PACK):
@@ -215,8 +221,8 @@ def tile_list_panel_transition_inks_kernel(
         for a in range(2):
             gb = tile("gb3_%d" % a, [P, PACK * N3], BF16, "hold%d" % a)
             nc.scalar.activation(
-                out=gb[:].rearrange("p (c i j) -> p c j i", i=4, j=PACK),
-                in_=raw3[a][:].rearrange("p j (c i) -> p c j i", i=4),
+                out=gb[:].rearrange("p (c i j) -> p c j i", i=2, j=PACK),
+                in_=raw3[a][:].rearrange("p j (c i) -> p c j i", i=2),
                 func=ACT.Copy,
             )
             w3q.append(quantise("w3q%d" % a, gb, N3))
@@ -251,6 +257,7 @@ def tile_list_panel_transition_inks_kernel(
 
         def finish(c, zq1):
             j0, width = CHUNKS[c]
+            done = []
             for gc, kind, n0, per, acc in groups:
                 if gc != c:
                     continue
@@ -261,6 +268,9 @@ def tile_list_panel_transition_inks_kernel(
                     nc.scalar.activation(out=res[:], in_=acc[:], func=ACT.Gelu_apprx_tanh)
                 else:
                     nc.scalar.activation(out=res[:], in_=acc[:], func=ACT.Tanh, scale=0.5)
+                done.append((kind, n0, per, res))
+            for kind, n0, per, res in done:
+                if kind == 1:
                     if c == len(CHUNKS) - 1:
                         nc.vector.tensor_scalar(out=res[:], in0=res[:], scalar1=0.5, scalar2=0.5, op0=ALU.mult, op1=ALU.add)
                     else:
@@ -271,31 +281,26 @@ def tile_list_panel_transition_inks_kernel(
                     in_=res[:].rearrange("p (k c) -> p k c", k=per),
                 )
 
-        nxt = [tile("nxt1_%d" % c, [P, PACK * w], F32) for c, (j, w) in enumerate(CHUNKS)]
+        nxt1 = tile("nxt1", [P, PACK * PAIRS], F32)
 
-        def pick1(which, c, t, dst):
-            pick(which, 1, t, CHUNKS[c][0], CHUNKS[c][1], dst)
+        def pick_prev(c, t, dst):
+            pick(0, 1, t, CHUNKS[c][0], CHUNKS[c][1], dst)
+
+        def join1(c, prev):
+            return join("z1_%d" % c, CHUNKS[c][1], prev, nxt1, CHUNKS[c][0], "hold0" if c == 0 else None)
 
         prev = tile("prev1_0", [P, PACK * CHUNKS[0][1]], F32)
         for t in range(PACK):
-            pick1(0, 0, t, prev)
-            pick1(1, 0, t, nxt[0])
-        pick1(1, 1, 0, nxt[1])
-        zb = join("z1_0", CHUNKS[0][1], prev, nxt[0])
-        pick1(1, 1, 1, nxt[1])
-        finish(0, quantise("z1_0", zb, CHUNKS[0][1]))
-        for t in range(2, PACK):
-            pick1(1, 1, t, nxt[1])
-        for t in range(PACK):
-            pick1(1, 2, t, nxt[2])
+            pick_prev(0, t, prev)
+            pick(1, 1, t, 0, PAIRS, nxt1)
+        finish(0, quantise("z1_0", join1(0, prev), CHUNKS[0][1]))
         prev = tile("prev1_1", [P, PACK * CHUNKS[1][1]], F32, "hold1")
         for t in range(PACK):
-            pick1(0, 1, t, prev)
-        zb = join("z1_1", CHUNKS[1][1], prev, nxt[1])
+            pick_prev(1, t, prev)
+        zb = join1(1, prev)
         prev = tile("prev1_2", [P, PACK * CHUNKS[2][1]], F32, "hold1")
-        pick1(0, 2, 0, prev)
+        pick_prev(2, 0, prev)
         finish(1, quantise("z1_1", zb, CHUNKS[1][1]))
         for t in range(1, PACK):
-            pick1(0, 2, t, prev)
-        zb = join("z1_2", CHUNKS[2][1], prev, nxt[2])
-        finish(2, quantise("z1_2", zb, CHUNKS[2][1]))
+            pick_prev(2, t, prev)
+        finish(2, quantise("z1_2", join1(2, prev), CHUNKS[2][1]))

@@ -101,12 +101,10 @@ def tile_list_panel_transition_inks_kernel(
 
         vw = {}
 
-        def gather_words(a, tag):
-            vw[a] = tile("vw%d" % a, [P, S], U16, tag)
+        def gather_words(a, tags):
             for u in range(2):
-                nc.vector.tensor_copy(
-                    out=vw[a][:, BANK * u : BANK * (u + 1)], in_=tabw[a][:].indirect(offs_t[:, 32 * u : 32 * (u + 1)])
-                )
+                vw[a, u] = tile("vw%d%d" % (a, u), [P, BANK], U16, tags[u])
+                nc.vector.tensor_copy(out=vw[a, u][:], in_=tabw[a][:].indirect(offs_t[:, 32 * u : 32 * (u + 1)]))
 
         plane0 = tile("plane0", [P, S], U8)
         nc.vector.tensor_copy(out=plane0[:], in_=tabs[:].indirect(offs_t[:]))
@@ -114,14 +112,14 @@ def tile_list_panel_transition_inks_kernel(
             nc.sync.dma_start(out=plane1[r:P:32, :].bitcast(I32), in_=plane0[16 + r : P : 32, :].bitcast(I32))
         planes = [plane0, plane1]
         load_blend(0, 0, 2, "tabs")
-        gather_words(0, None)
+        gather_words(0, (None, None))
         ng = tile("ng", [P, 2, PACK], F32)
         nc.gpsimd.tensor_scalar(out=ng[:], in0=g[:], scalar1=-1.0, scalar2=None, op0=ALU.mult)
         gb00 = tile("gb00", [P, PACK * PASS], BF16)
         cast_w1(raw00, gb00, 0, P)
         w1q = {}
         w1q[0, 0] = quantise("w1q00", gb00, PASS)
-        gather_words(1, "gb00")
+        gather_words(1, (None, "gb00"))
         gb10 = tile("gb10", [P, PACK * PASS], BF16)
         for u in range(2):
             cast_w1(raw10[u], gb10, 64 * u, 64 * (u + 1))
@@ -136,16 +134,17 @@ def tile_list_panel_transition_inks_kernel(
             ht = tile("h%d%d" % (b, t), [P, S], F32)
             for u in range(2):
                 acc = bank((2 * t + u) % 4, "acc%d%d%d" % (b, t, u))
-                for a in range(2):
+                order = (0, 1) if t == 0 else (1, 0)
+                for a in order:
                     codes, scales = w1q[a, b]
                     nc.tensor.matmul_mx(
                         out=acc[:],
                         lhsT=codes[:, P * t : P * (t + 1)].bitcast(FP8X4),
                         lhsT_scale=scales[:, P * t : P * (t + 1)],
-                        rhs=vw[a][:, BANK * u : BANK * (u + 1)].bitcast(FP4X4),
+                        rhs=vw[a, u][:].bitcast(FP4X4),
                         rhs_scale=planes[a][:, BANK * u : BANK * (u + 1)],
-                        start=(a == 0),
-                        stop=(a == 1),
+                        start=(a == order[0]),
+                        stop=(a == order[1]),
                     )
                 nc.scalar.activation(out=ht[:, BANK * u : BANK * (u + 1)], in_=acc[:], func=ACT.Tanh)
             h[b, t] = ht
@@ -174,14 +173,16 @@ def tile_list_panel_transition_inks_kernel(
                 op=ALU.mult,
             )
 
-        def join(name, width, prev, nxt, j0, tag=None):
+        def join(name, width, prev, nxt, j0, tag=None, parts=1):
             zb = tile(name + "_b", [P, PACK * width], BF16, tag)
-            nc.vector.tensor_tensor(
-                out=zb[:].rearrange("p (c i t) -> p c t i", i=2, t=PACK),
-                in0=prev[:].rearrange("p (t c i) -> p c t i", t=PACK, i=2),
-                in1=nxt[:].rearrange("p (t c i) -> p c t i", t=PACK, i=2)[:, j0 // 2 : (j0 + width) // 2],
-                op=ALU.add,
-            )
+            step = width // 2 // parts
+            for c0 in range(0, width // 2, step):
+                nc.vector.tensor_tensor(
+                    out=zb[:].rearrange("p (c i t) -> p c t i", i=2, t=PACK)[:, c0 : c0 + step],
+                    in0=prev[:].rearrange("p (t c i) -> p c t i", t=PACK, i=2)[:, c0 : c0 + step],
+                    in1=nxt[:].rearrange("p (t c i) -> p c t i", t=PACK, i=2)[:, j0 // 2 + c0 : j0 // 2 + c0 + step],
+                    op=ALU.add,
+                )
             return zb
 
         prev0 = tile("prev0", [P, PACK * PAIRS], F32)
@@ -263,12 +264,15 @@ def tile_list_panel_transition_inks_kernel(
                     continue
                 for k in range(per):
                     second(kind, n0 + k, 1, acc, width * k, zq1, 0, width, False, k == per - 1)
-                res = tile("res%d%d%d" % (c, kind, n0), [P, BANK], F32)
-                if kind == 0:
-                    nc.scalar.activation(out=res[:], in_=acc[:], func=ACT.Gelu_apprx_tanh)
-                else:
-                    nc.scalar.activation(out=res[:], in_=acc[:], func=ACT.Tanh, scale=0.5)
-                done.append((kind, n0, per, res))
+                parts = 2 if c == len(CHUNKS) - 1 else 1
+                for half in range(parts):
+                    cols = slice(BANK // parts * half, BANK // parts * (half + 1))
+                    res = tile("res%d%d%d%d" % (c, kind, n0, half), [P, BANK // parts], F32)
+                    if kind == 0:
+                        nc.scalar.activation(out=res[:], in_=acc[:, cols], func=ACT.Gelu_apprx_tanh)
+                    else:
+                        nc.scalar.activation(out=res[:], in_=acc[:, cols], func=ACT.Tanh, scale=0.5)
+                    done.append((kind, n0 + per // parts * half, per // parts, res))
             for kind, n0, per, res in done:
                 if kind == 1:
                     if c == len(CHUNKS) - 1:
@@ -287,7 +291,7 @@ def tile_list_panel_transition_inks_kernel(
             pick(0, 1, t, CHUNKS[c][0], CHUNKS[c][1], dst)
 
         def join1(c, prev):
-            return join("z1_%d" % c, CHUNKS[c][1], prev, nxt1, CHUNKS[c][0], "hold0" if c == 0 else None)
+            return join("z1_%d" % c, CHUNKS[c][1], prev, nxt1, CHUNKS[c][0], "hold0" if c == 0 else None, 2 if c == 2 else 1)
 
         prev = tile("prev1_0", [P, PACK * CHUNKS[0][1]], F32)
         for t in range(PACK):
@@ -303,4 +307,4 @@ def tile_list_panel_transition_inks_kernel(
         finish(1, quantise("z1_1", zb, CHUNKS[1][1]))
         for t in range(1, PACK):
             pick_prev(2, t, prev)
-        finish(2, quantise("z1_2", join1(2, prev), CHUNKS[2][1]))
+        finish(2, quantise("z1_2", join1(2, prev), CHUNKS[2][1], (64,)))

from contextlib import ExitStack

import concourse.mybir as mybir

K, T, S, H, PAIRS, N2, N3 = 1024, 2048, 1024, 1024, 512, 512, 512
FLOPS = 2 * K * H * S + 2 * H * (N2 + N3) * PAIRS

F32 = mybir.dt.float32
BF16 = mybir.dt.bfloat16
I32 = mybir.dt.int32
U32 = mybir.dt.uint32
U16 = mybir.dt.uint16
U8 = mybir.dt.uint8
FP8X4 = mybir.dt.float8_e4m3fn_x4
FP4X4 = mybir.dt.float4_e2m1fn_x4
ACT = mybir.ActivationFunctionType
ALU = mybir.AluOpType

P = 128
PACK = 4
PASS = P * PACK
BANK = 512
CHUNKS = ((0, 256), (256, 128), (384, 128))


def tile_list_panel_transition_inks_kernel(
    tc, tab_words, tab_scales, offs, pos1, pos2, w1, gain, blend, w2_words, w2_scales, w3, out
):
    nc = tc.nc
    with ExitStack() as ctx:
        lists = ctx.enter_context(tc.tile_pool(name="lists", bufs=1))
        sb = ctx.enter_context(tc.tile_pool(name="sb", bufs=1))
        psum = ctx.enter_context(tc.psum_pool(name="psum", bufs=1))

        def tile(name, shape, dtype, tag=None):
            return sb.tile(shape, dtype, name=name, tag=tag or name, align_bytes=64)

        def bank(i, name):
            return psum.tile([P, BANK], F32, name=name, tag="bank%d" % i)

        offs_t = lists.tile([P, S // 16], U16, name="offs_t")
        pos1_t = lists.tile([P, PAIRS // 16], U16, name="pos1_t")
        pos2_t = lists.tile([P, PAIRS // 16], U16, name="pos2_t")

        tabw = [tile("tabw%d" % a, [P, T], U16) for a in range(2)]
        tabs = tile("tabs", [P, T], U8)
        plane1 = tile("plane1", [P, S], U8)
        nc.gpsimd.memset(tabs[:].bitcast(I32), 0)
        nc.vector.memset(plane1[:].bitcast(I32), 0)
        g = tile("g", [P, 2, PACK], F32)
        nc.gpsimd.dma_start(out=g[:], in_=gain.rearrange("(b p t) -> p b t", b=2, t=PACK))

        def load_w1(a, b, c0, c1, name, tag=None):
            raw = tile(name, [P, PACK, c1 - c0], F32, tag)
            nc.sync.dma_start(
                out=raw[:],
                in_=w1[PASS * a : PASS * (a + 1), PASS * b + c0 : PASS * b + c1].rearrange("(p j) c -> p j c", j=PACK),
            )
            return raw

        def load_blend(b, t0, t1, tag=None):
            rows = tile("blend%d%d" % (b, t0), [P, (t1 - t0) * PAIRS], F32, tag)
            nc.sync.dma_start(
                out=rows[:],
                in_=blend[PASS * b : PASS * (b + 1), :].rearrange("(p t) j -> p (t j)", t=PACK)[:, PAIRS * t0 : PAIRS * t1],
            )
            for t in range(t0, t1):
                wa[b, t] = rows[:, PAIRS * (t - t0) : PAIRS * (t - t0 + 1)]

        nc.sync.dma_start(out=offs_t[:], in_=offs)
        nc.sync.dma_start(out=tabw[0][:].bitcast(I32), in_=tab_words[0].bitcast(I32))
        for r in range(4):
            nc.sync.dma_start(
                out=tabs[r:P:16, :].bitcast(I32), in_=tab_scales[:, r:16:4, :].rearrange("a q t -> q a t").bitcast(I32)
            )
        raw00 = load_w1(0, 0, 0, PASS, "raw00")
        nc.sync.dma_start(out=tabw[1][:].bitcast(I32), in_=tab_words[1].bitcast(I32))
        raw10 = [load_w1(1, 0, 256 * u, 256 * (u + 1), "raw10_%d" % u) for u in range(2)]
        nc.sync.dma_start(out=pos1_t[:], in_=pos1)
        nc.sync.dma_start(out=pos2_t[:], in_=pos2)
        wa = {}
        load_blend(0, 2, 4)

        def cast_w1(raw, grouped, m0, m1):
            for v in range(2):
                nc.scalar.activation(
                    out=grouped[:].rearrange("p (v e m j) -> p v m j e", v=2, e=2, j=PACK)[:, v, m0:m1],
                    in_=raw[:].rearrange("p j (m v e) -> p v m j e", v=2, e=2)[:, v],
                    func=ACT.Copy,
                )

        def quantise(name, grouped, width, cuts=()):
            codes = tile(name + "_c", [P, width], U32)
            scales = tile(name + "_s", [P, width], U8)
            edges = (0,) + cuts + (width,)
            for c0, c1 in zip(edges, edges[1:]):
                nc.vector.quantize_mx(
                    out=codes[:, c0:c1].bitcast(FP8X4), scales=scales[:, c0:c1], in_=grouped[:, PACK * c0 : PACK * c1]
                )
            return codes, scales

        vw = {}

        def gather_words(a, tags):
            for u in range(2):
                vw[a, u] = tile("vw%d%d" % (a, u), [P, BANK], U16, tags[u])
                nc.vector.tensor_copy(out=vw[a, u][:], in_=tabw[a][:].indirect(offs_t[:, 32 * u : 32 * (u + 1)]))

        plane0 = tile("plane0", [P, S], U8)
        nc.vector.tensor_copy(out=plane0[:], in_=tabs[:].indirect(offs_t[:]))
        for r in range(4):
            nc.sync.dma_start(out=plane1[r:P:32, :].bitcast(I32), in_=plane0[16 + r : P : 32, :].bitcast(I32))
        planes = [plane0, plane1]
        load_blend(0, 0, 2, "tabs")
        gather_words(0, (None, None))
        ng = tile("ng", [P, 2, PACK], F32)
        nc.gpsimd.tensor_scalar(out=ng[:], in0=g[:], scalar1=-1.0, scalar2=None, op0=ALU.mult)
        gb00 = tile("gb00", [P, PACK * PASS], BF16)
        cast_w1(raw00, gb00, 0, P)
        w1q = {}
        w1q[0, 0] = quantise("w1q00", gb00, PASS)
        gather_words(1, (None, "gb00"))
        gb10 = tile("gb10", [P, PACK * PASS], BF16)
        for u in range(2):
            cast_w1(raw10[u], gb10, 64 * u, 64 * (u + 1))
        w1q[1, 0] = quantise("w1q10", gb10, PASS, (P,))
        raw01 = load_w1(0, 1, 0, PASS, "raw01", "raw00")
        raw11 = load_w1(1, 1, 0, PASS, "raw11", "raw10_0")
        load_blend(1, 0, 4, "tabw1")

        h = {}

        def features(b, t):
            ht = tile("h%d%d" % (b, t), [P, S], F32)
            for u in range(2):
                acc = bank((2 * t + u) % 4, "acc%d%d%d" % (b, t, u))
                order = (0, 1) if t == 0 else (1, 0)
                for a in order:
                    codes, scales = w1q[a, b]
                    nc.tensor.matmul_mx(
                        out=acc[:],
                        lhsT=codes[:, P * t : P * (t + 1)].bitcast(FP8X4),
                        lhsT_scale=scales[:, P * t : P * (t + 1)],
                        rhs=vw[a, u][:].bitcast(FP4X4),
                        rhs_scale=planes[a][:, BANK * u : BANK * (u + 1)],
                        start=(a == order[0]),
                        stop=(a == order[1]),
                    )
                nc.scalar.activation(out=ht[:, BANK * u : BANK * (u + 1)], in_=acc[:], func=ACT.Tanh)
            h[b, t] = ht

        mix = {}
        early = tile("early", [P, 4 * PAIRS], F32, "gb10")

        def weights(b, t):
            gt, ngt = g[:, b, t : t + 1], ng[:, b, t : t + 1]
            if b == 0 and t < 2:
                wp, wn = (early[:, PAIRS * (2 * t + w) : PAIRS * (2 * t + w + 1)] for w in range(2))
                nc.vector.tensor_scalar(out=wp, in0=wa[b, t], scalar1=gt, scalar2=None, op0=ALU.mult)
                nc.vector.tensor_scalar(out=wn, in0=wa[b, t], scalar1=ngt, scalar2=gt, op0=ALU.mult, op1=ALU.add)
            else:
                both = tile("mix%d%d" % (b, t), [P, 2 * PAIRS], F32, {(0, 2): "raw10_1", (0, 3): "tabs"}.get((b, t)))
                wp, wn = both[:, 0:PAIRS], both[:, PAIRS : 2 * PAIRS]
                nc.scalar.activation(out=wp, in_=wa[b, t], func=ACT.Copy, scale=gt)
                nc.scalar.activation(out=wn, in_=wa[b, t], func=ACT.Identity, bias=gt, scale=ngt)
            mix[0, b, t], mix[1, b, t] = wp, wn

        def pick(which, b, t, j0, width, dst):
            nc.vector.tensor_tensor(
                out=dst[:, width * t : width * (t + 1)],
                in0=h[b, t][:].indirect((pos1_t, pos2_t)[which][:, j0 // 16 : (j0 + width) // 16]),
                in1=mix[which, b, t][:, j0 : j0 + width],
                op=ALU.mult,
            )

        def join(name, width, prev, nxt, j0, tag=None, parts=1):
            zb = tile(name + "_b", [P, PACK * width], BF16, tag)
            step = width // 2 // parts
            for c0 in range(0, width // 2, step):
                nc.vector.tensor_tensor(
                    out=zb[:].rearrange("p (c i t) -> p c t i", i=2, t=PACK)[:, c0 : c0 + step],
                    in0=prev[:].rearrange("p (t c i) -> p c t i", t=PACK, i=2)[:, c0 : c0 + step],
                    in1=nxt[:].rearrange("p (t c i) -> p c t i", t=PACK, i=2)[:, j0 // 2 + c0 : j0 // 2 + c0 + step],
                    op=ALU.add,
                )
            return zb

        prev0 = tile("prev0", [P, PACK * PAIRS], F32)
        nxt0 = tile("nxt0", [P, PACK * PAIRS], F32)
        for t in range(PACK):
            features(0, t)
            weights(0, t)
            pick(0, 0, t, 0, PAIRS, prev0)
            pick(1, 0, t, 0, PAIRS, nxt0)
            if t in (1, 2):
                a = t - 1
                gb = tile("gb%d1" % a, [P, PACK * PASS], BF16)
                cast_w1((raw01, raw11)[a], gb, 0, P)
                w1q[a, 1] = quantise("w1q%d1" % a, gb, PASS)
        zq0 = quantise("z0", join("z0", PAIRS, prev0, nxt0, 0), PAIRS)

        raw3 = []
        for a in range(2):
            raw = tile("raw3_%d" % a, [P, PACK, N3], F32, "gb10" if a == 0 else "raw00")
            nc.sync.dma_start(out=raw[:], in_=w3[PASS * a : PASS * (a + 1), :].rearrange("(p j) n -> p j n", j=PACK))
            raw3.append(raw)
        w2s = tile("w2s", [P, 2 * N2], U8, "gb01")
        nc.gpsimd.memset(w2s[:].bitcast(I32), 0)
        for q in range(4):
            nc.sync.dma_start(
                out=w2s[32 * q : 32 * q + 4, :].rearrange("r (a n) -> r a n", a=2).bitcast(I32),
                in_=w2_scales[:, 4 * q : 4 * q + 4, :].rearrange("a r n -> r a n").bitcast(I32),
            )
        w2w = tile("w2w", [P, 2, 2 * N2], U8, "gb11")
        nc.sync.dma_start(out=w2w[:].bitcast(I32), in_=w2_words.rearrange("a p c -> p a c").bitcast(I32))

        for t in range(PACK):
            weights(1, t)
            features(1, t)

        w3q = []
        for a in range(2):
            gb = tile("gb3_%d" % a, [P, PACK * N3], BF16, "hold%d" % a)
            nc.scalar.activation(
                out=gb[:].rearrange("p (c i j) -> p c j i", i=2, j=PACK),
                in_=raw3[a][:].rearrange("p j (c i) -> p c j i", i=2),
                func=ACT.Copy,
            )
            w3q.append(quantise("w3q%d" % a, gb, N3))

        def second(kind, n, a, acc, c0, zq, z0, width, start, stop):
            codes, scales = zq
            if kind == 0:
                lhsT = w2w[:, a, 2 * P * n : 2 * P * (n + 1)].bitcast(FP4X4)
                lhsT_scale = w2s[:, N2 * a + P * n : N2 * a + P * (n + 1)]
            else:
                lhsT = w3q[a][0][:, P * n : P * (n + 1)].bitcast(FP8X4)
                lhsT_scale = w3q[a][1][:, P * n : P * (n + 1)]
            nc.tensor.matmul_mx(
                out=acc[:, c0 : c0 + width],
                lhsT=lhsT,
                lhsT_scale=lhsT_scale,
                rhs=codes[:, z0 : z0 + width].bitcast(FP8X4),
                rhs_scale=scales[:, z0 : z0 + width],
                start=start,
                stop=stop,
            )

        groups = []
        for c, (j0, width) in enumerate(CHUNKS):
            per = BANK // width
            for kind in (1, 0):
                for n0 in range(0, 4, per):
                    acc = bank((len(groups) + 4) % 8, "out%d%d%d" % (c, kind, n0))
                    groups.append((c, kind, n0, per, acc))
                    for k in range(per):
                        second(kind, n0 + k, 0, acc, width * k, zq0, j0, width, k == 0, False)

        def finish(c, zq1):
            j0, width = CHUNKS[c]
            done = []
            for gc, kind, n0, per, acc in groups:
                if gc != c:
                    continue
                for k in range(per):
                    second(kind, n0 + k, 1, acc, width * k, zq1, 0, width, False, k == per - 1)
                parts = 2 if c == len(CHUNKS) - 1 else 1
                for half in range(parts):
                    cols = slice(BANK // parts * half, BANK // parts * (half + 1))
                    res = tile("res%d%d%d%d" % (c, kind, n0, half), [P, BANK // parts], F32)
                    if kind == 0:
                        nc.scalar.activation(out=res[:], in_=acc[:, cols], func=ACT.Gelu_apprx_tanh)
                    else:
                        nc.scalar.activation(out=res[:], in_=acc[:, cols], func=ACT.Tanh, scale=0.5)
                    done.append((kind, n0 + per // parts * half, per // parts, res))
            for kind, n0, per, res in done:
                if kind == 1:
                    if c == len(CHUNKS) - 1:
                        nc.vector.tensor_scalar(out=res[:], in0=res[:], scalar1=0.5, scalar2=0.5, op0=ALU.mult, op1=ALU.add)
                    else:
                        nc.scalar.activation(out=res[:], in_=res[:], func=ACT.Copy, scale=0.5, bias=0.5)
                row0 = N2 * kind + P * n0
                nc.sync.dma_start(
                    out=out[row0 : row0 + P * per, j0 : j0 + width].rearrange("(k p) c -> p k c", p=P),
                    in_=res[:].rearrange("p (k c) -> p k c", k=per),
                )

        nxt1 = tile("nxt1", [P, PACK * PAIRS], F32)

        def pick_prev(c, t, dst):
            pick(0, 1, t, CHUNKS[c][0], CHUNKS[c][1], dst)

        def join1(c, prev):
            return join("z1_%d" % c, CHUNKS[c][1], prev, nxt1, CHUNKS[c][0], "hold0" if c == 0 else None, 2 if c == 2 else 1)

        prev = tile("prev1_0", [P, PACK * CHUNKS[0][1]], F32)
        for t in range(PACK):
            pick_prev(0, t, prev)
            pick(1, 1, t, 0, PAIRS, nxt1)
        finish(0, quantise("z1_0", join1(0, prev), CHUNKS[0][1]))
        prev = tile("prev1_1", [P, PACK * CHUNKS[1][1]], F32, "hold1")
        for t in range(PACK):
            pick_prev(1, t, prev)
        zb = join1(1, prev)
        prev = tile("prev1_2", [P, PACK * CHUNKS[2][1]], F32, "hold1")
        pick_prev(2, 0, prev)
        finish(1, quantise("z1_1", zb, CHUNKS[1][1]))
        for t in range(1, PACK):
            pick_prev(2, t, prev)
        finish(2, quantise("z1_2", join1(2, prev), CHUNKS[2][1], (64,)))
